import numpy as np, ml_dtypes
CORES = [3,7,11,15,131,135,139,143]
N = 8
BF = ml_dtypes.bfloat16
def gentries(a):
    return np.ascontiguousarray(a.reshape(8, 16, -1).transpose(0, 2, 1)).reshape(8, -1)
def gtable(e):
    e = np.asarray(e); return np.ascontiguousarray(e.reshape(8, -1, 16).transpose(0, 2, 1)).reshape(128, -1).astype(np.int32)
def f(rng, *shape):
    return (rng.standard_normal(shape, dtype=np.float32) * np.exp2(rng.integers(-2, 3, shape[:-1] + (1,)))).astype(BF)
def wide(rng, *shape):
    v = f(rng, *shape).astype(np.float32); k = shape[:-2] + (1, shape[-1])
    return (v * np.exp2(rng.integers(-6, 7, k)) * (rng.random(k) > 0.0625)).astype(BF)
M, A, L, C, SR, SA = 2048, 512, 3, 4, 128, 64
def first(l):
    return M + N * SR + (l - 1) * (A + N * SA)
def glists(e):
    return np.stack([gtable(e[r].reshape(8, -1)) for r in range(N)])
def grow(rng, n):
    v = rng.standard_exponential((N, 8, 16, n), dtype=np.float32) * (rng.random((N, 8, 16, n)) < 0.75) * (0.5 + rng.random((N, 8, 1, n)))
    return np.add.accumulate(v, axis=2).reshape(N, 128, n).astype(BF)
def draw_parts(rng):
    e = np.zeros((N, 8, L, 2 * C, A), np.int64); k = (N, 8, 2 * C, A)
    for l in range(1, L + 1):
        e[:, :, l - 1] = rng.integers(0, first(l), k)
        if l > 1: e[:, :, l - 1] = np.where(rng.random(k) < 0.5, rng.integers(first(l - 1), first(l), k), e[:, :, l - 1])
    return e
def draw(rng, e):
    return {"sup": grow(rng, M), "cap": grow(rng, L * A), "stock": (8 * rng.random((N, 128, L * A)) * (rng.random((N, 128, L * A)) < 0.8)).astype(BF), "parts": glists(e),
            "ship": glists(rng.integers(0, M, (N, 8, N * SR))), "hand": glists(rng.integers(0, A, (N, 8, (L - 1) * N * SA)))}
def setup_inputs(rng):
    return draw(rng, draw_parts(rng))
def setup_inputs_ties(rng):
    e = draw_parts(rng); e[:, :, :, 1:C] = np.where(rng.random((N, 8, L, C - 1, A)) < 0.3, e[:, :, :, :1], e[:, :, :, 1:C])
    e[:, :, :, C:] = np.where(rng.random((N, 8, L, C, A)) < 0.2, e[:, :, :, :C], e[:, :, :, C:])
    d = draw(rng, e)
    d["sup"] = np.add.accumulate(rng.integers(0, 2, (N, 8, 16, M)), axis=2).reshape(N, 128, M).astype(np.float32).astype(BF)
    d["cap"] = np.add.accumulate(rng.integers(0, 3, (N, 8, 16, L * A)), axis=2).reshape(N, 128, L * A).astype(np.float32).astype(BF)
    d["stock"] = rng.integers(0, 4, (N, 128, L * A)).astype(np.float32).astype(BF); return d
def setup_inputs_ends(rng):
    e = draw_parts(rng)
    for l in range(1, L + 1):
        b = [0, M - 1, M, M + N * SR - 1]
        for m in range(1, l): b += [first(m), first(m) + A - 1, first(m) + A, first(m + 1) - 1]
        k = (N, 8, 2 * C, A); e[:, :, l - 1] = np.where(rng.random(k) < 0.5, rng.choice(np.array(b), k), e[:, :, l - 1])
        for r in range(N):
            q = (r + 1) % N
            for g in range(8):
                if l == 1: e[r, g, 0, 0, :SR] = M + q * SR + rng.permutation(SR)
                else: e[r, g, l - 1, 0, :SA] = first(l - 1) + A + q * SA + rng.permutation(SA)
    d = draw(rng, e)
    s = rng.integers(0, M, (N, 8, N, SR)); s[..., 0] = 0; s[..., -1] = M - 1; d["ship"] = glists(s)
    h = rng.integers(0, A, (N, 8, L - 1, N, SA)); h[..., 0] = A - 1; h[..., -1] = 0; d["hand"] = glists(h); return d
def setup_inputs_one(rng):
    e = np.zeros((N, 8, L, 2 * C, A), np.int64); a = rng.integers(1, N); k = (8, 2 * C, A)
    for r in range(N):
        q = (r + a) % N; e[r, :, 0] = M + q * SR + rng.integers(0, SR, k)
        for l in range(2, L + 1): e[r, :, l - 1] = first(l - 1) + A + q * SA + rng.integers(0, SA, k)
    d = draw(rng, e); s = rng.integers(0, M, (N, 8, N, SR)); q = rng.integers(0, N); s[q] = s[q][..., :1]; d["ship"] = glists(s); return d
def setup_inputs_late(rng):
    d = setup_inputs(rng); v = d["sup"].astype(np.float32).reshape(N, 8, 16, M); v[:, :, 15] = 64 - v[:, :, 14]; d["sup"] = v.reshape(N, 128, M).astype(BF)
    c = d["cap"].astype(np.float32).reshape(N, 8, 16, L * A); t = rng.integers(0, 14, (N, 8, 1, L * A))
    d["cap"] = np.where(np.arange(16)[:, None] < t - 4, np.float32(0), 8 * c).reshape(N, 128, L * A).astype(BF); return d
def setup_inputs_spread(rng):
    d = setup_inputs(rng)
    for k, n in (("sup", M), ("cap", L * A), ("stock", L * A)): d[k] = (wide(rng, N, 128, n).astype(np.float32) * np.float32(2.0 ** 40)).astype(BF)
    return d
def check_inputs(d):
    bad = []
    try:
        for k in ("sup", "cap", "stock"):
            v = d[k].astype(np.float32)
            if not (np.isfinite(v).all() and (np.abs(v) <= 2.0 ** 60).all()): bad.append(k)
        e = np.stack([gentries(v) for v in d["parts"]]).reshape(N, 8, L, 2 * C * A)
        if any((e[:, :, l - 1] < 0).any() or (e[:, :, l - 1] >= first(l)).any() for l in range(1, L + 1)): bad.append("parts")
        for k, n in (("ship", M), ("hand", A)):
            if (d[k] < 0).any() or (d[k] >= n).any(): bad.append(k)
    except Exception:
        bad.append("shapes")
    return bad
def reference(sup, cap, stock, parts, ship, hand):
    raw = sup.astype(np.float32).reshape(N, 8, 16, M); ca = cap.astype(np.float32).reshape(N, 8, 16, L, A); st = stock.astype(np.float32).reshape(N, 8, 16, L, A)
    e = [gentries(v).reshape(8, L, 1, 2 * C * A) for v in parts]; sh = [gentries(v).reshape(8, 1, N, SR) for v in ship]; ha = [gentries(v).reshape(8, 1, L - 1, N, SA) for v in hand]
    w = np.zeros((N, 8, 16, first(L)), np.float32); now = np.zeros((N, 8, 16, A), np.float32)
    w[..., :M] = raw; h = A // 2
    for r in range(N):
        for q in range(N): w[r, :, :, M + q * SR:M + (q + 1) * SR] = np.take_along_axis(raw[q], sh[q][:, :, r], 2)
    for l in range(1, L + 1):
        for r in range(N):
            v = np.take_along_axis(w[r], e[r][:, l - 1], 2).reshape(8, 16, 2 * C, A)
            i = np.argmin(v[:, 15, :C], axis=1)
            hit = np.arange(C)[:, None] == i[:, None]
            z = np.min(np.where(hit[:, None], v[:, :, C:], v[:, :, :C]), axis=2)
            s = np.zeros_like(z); s[:, 1:, :h] = z[:, :-1, :h]; s[:, 2:, h:] = z[:, :-2, h:]
            now[r] = np.minimum(s, ca[r, :, :, l - 1]) + st[r, :, :, l - 1]
        if l < L:
            b = first(l); w[:, :, :, b:b + A] = now
            for r in range(N):
                for q in range(N): w[r, :, :, b + A + q * SA:b + A + (q + 1) * SA] = np.take_along_axis(now[q], ha[q][:, :, l - 1, r], 2)
    return {"y": now.reshape(N, 128, A)}

@@ -1,0 +1,293 @@
+import numpy as np
+from concourse.bass import DstId, RemoteDMATransfer
+from concourse.mybir import AluOpType as OP, ActivationFunctionType as AF
+
+M, A, L, SR, SA, N = 2048, 512, 3, 128, 64, 8
+H = A // 2
+
+
+def first(l):
+    return M + N * SR + (l - 1) * (A + N * SA)
+
+
+BF, F32, I32, U16 = "bfloat16", "float32", "int32", "uint16"
+SCRATCH = {
+    "WB": ("sbuf", [128, M + N * SR], BF),
+    "W": ("sbuf", [128, first(L)], F32),
+    "shipi": ("sbuf", [128, 64], I32), "handi": ("sbuf", [128, 64], I32),
+    "ship16": ("sbuf", [128, 64], U16), "hand16": ("sbuf", [128, 64], U16),
+    "PT": ("sbuf", [128, 768], I32), "cu": ("sbuf", [128, 384], U16),
+    "cf": ("sbuf", [128, 384], F32), "df": ("sbuf", [128, 384], F32),
+    "SB": ("sbuf", [128, N * SR], BF), "SH1": ("sbuf", [128, N * SA], F32), "SH2": ("sbuf", [128, N * SA], F32),
+    "GB": ("sbuf", [128, 2048], BF), "DB": ("sbuf", [128, 2048], BF),
+    "GF": ("sbuf", [128, 2048], F32), "DF": ("sbuf", [128, 2048], F32),
+    "Bt": ("sbuf", [128, 64], BF), "Mt": ("sbuf", [128, 64], F32), "Gt": ("sbuf", [128, 64], BF), "Hd": ("sbuf", [128, 128], BF),
+    "SI": ("sbuf", [128, 128], F32), "sel": ("sbuf", [128, 128], U16),
+    "XB0": ("sbuf", [128, A], BF), "XB1": ("sbuf", [128, A], BF), "XF0": ("sbuf", [128, A], F32), "XF1": ("sbuf", [128, A], F32),
+    "C1": ("sbuf", [128, L * A], BF), "C2": ("sbuf", [128, L * A], BF), "MC": ("sbuf", [128, L * A], BF), "ST": ("sbuf", [128, L * A], BF),
+    "YB": ("sbuf", [128, A], F32),
+    "ones": ("sbuf", [128, 128], BF), "dist": ("sbuf", [128, 128], I32), "dm": ("sbuf", [128, 128], I32), "m16": ("sbuf", [128, 128], I32),
+    "a1": ("sbuf", [128, 128], BF), "a2": ("sbuf", [128, 128], BF), "k1": ("sbuf", [128, 128], BF), "k2": ("sbuf", [128, 128], BF),
+    "sb1": ("sbuf", [128, 128], BF), "sb2": ("sbuf", [128, 128], BF), "sf1": ("sbuf", [128, 128], F32), "sf2": ("sbuf", [128, 128], F32),
+    "e1": ("sbuf", [128, 128], BF), "e2": ("sbuf", [128, 128], BF), "idn": ("sbuf", [128, 128], BF),
+    "up": ("sbuf", [128, 128], BF), "dn": ("sbuf", [128, 128], BF),
+    "x00": ("sbuf", [128, 128], BF), "x01": ("sbuf", [128, 128], BF), "x10": ("sbuf", [128, 128], BF), "x11": ("sbuf", [128, 128], BF),
+    "PH": ("psum", [128, 512], F32), "TP": ("psum", [128, 512], F32),
+    "P0": ("psum", [128, 512], F32), "P1": ("psum", [128, 512], F32), "P2": ("psum", [128, 512], F32),
+}
+NPOOL = 125
+SEMAPHORES = ["arr0", "arr1", "arr2", "loc0", "loc1", "loc2"] + ["s%d" % i for i in range(NPOOL)]
+SLOT = {0: 0, 2: 1, 1: 2, 3: 3}
+PIECES = [(0, 256, 1), (256, 384, 2), (384, 512, 2)]
+
+
+def rank_program(g, core, T, topo):
+    rank = T.rank_of(core)
+    if rank is None:
+        return
+    Q = {"v": g.vector, "s": g.scalar, "t": g.tensor, "g": g, "y": g.sync}
+    pool, total, seen, best = {}, {}, {q: {} for q in Q}, {}
+
+    def wait(q, tok):
+        name, val = tok
+        if seen[q].get(name, 0) >= val:
+            return
+        Q[q].wait_ge(T.sem[name], val)
+        seen[q][name] = val
+        best[name] = max(best.get(name, 0), val)
+
+    def do(q, fn, role, deps, n=1):
+        for d in deps:
+            wait(q, d)
+        inst = fn()
+        if role is None:
+            return None
+        if role not in pool:
+            pool[role] = "s%d" % len(pool)
+        name = pool[role]
+        inst.then_inc(T.sem[name], n)
+        total[name] = total.get(name, 0) + n
+        return (name, total[name])
+
+    V, S, PE, SY = g.vector, g.scalar, g.tensor, g.sync
+
+    def tt(out, a, b, op, role, deps):
+        return do("v", lambda: V.tensor_tensor(out=out, in0=a, in1=b, op=op), role, deps)
+
+    def ts(out, a, s1, op, role, deps):
+        return do("v", lambda: V.tensor_scalar(out=out, in0=a, scalar1=s1, scalar2=None, op0=op), role, deps)
+
+    def vcopy(out, a, role, deps):
+        return do("v", lambda: V.tensor_copy(out=out, in_=a), role, deps)
+
+    def scopy(out, a, role, deps):
+        return do("s", lambda: S.activation(out=out, in_=a, func=AF.Copy), role, deps)
+
+    def dma(q, out, in_, role, deps=()):
+        return do(q, lambda: Q[q].dma_start(out=out, in_=in_), role, deps, 16)
+
+    here = topo.cores_of(core)
+    far = [r for r in range(N) if topo.host(T.cores[r]) != topo.host(core)]
+    buddy = [r for r in range(N) if T.cores[r] in here and r != rank]
+    near = [r for r in range(N) if r not in far and r not in buddy and r != rank]
+    off = topo.engines(core, T.cores[far[0]])
+    rest = [e for e in topo.engines(core, T.cores[buddy[0]]) if e not in off]
+    share = {}
+    for grp in (far, near):
+        k = len(off) // len(grp)
+        for j, r in enumerate(grp):
+            share[r] = off[j * k:(j + 1) * k]
+    for j, r in enumerate(buddy):
+        share[r] = rest[4 * j:4 * j + 4:2]
+    landed = sum(len(v) for v in share.values())
+
+    def send(ranks, src, dst, w_src, w_dst, k, deps):
+        for d in deps:
+            wait("g", d)
+        tr = []
+        for r in ranks:
+            rid, pid = topo.addr(T.cores[r], core)
+            tr.append(RemoteDMATransfer(src=src[:, r * w_src:(r + 1) * w_src], dst=dst[:, w_dst + rank * w_src:w_dst + (rank + 1) * w_src],
+                                        dst_ids=[DstId(rid=rid, pnc=pid)], dma_engine_mask=sum(1 << e for e in share[r]),
+                                        remote_sem=T.sem["arr%d" % k]))
+        g.remote_dma_fused(tr, local_sem=T.sem["loc%d" % k])
+
+    def runs(ranks):
+        out = []
+        for r in ranks:
+            if out and out[-1][1] == r:
+                out[-1][1] = r + 1
+            else:
+                out.append([r, r + 1])
+        return out
+
+    def hand_over(win, lists, col0, per, stage, dst, w_dst, k, deps):
+        per16 = per // 16
+        toks = {}
+
+        def pick(q, ranks, tag):
+            got = []
+            for j, (b, e) in enumerate(runs(ranks)):
+                o, i = stage[:, b * per:e * per], win.indirect(lists[:, col0 + b * per16:col0 + e * per16])
+                got.append((vcopy if q == "v" else scopy)(o, i, "hand%s%s%d" % (q, tag, j), deps))
+            return got
+        h = len(far) // 2
+        t1 = pick("v", far[:h], "f") + pick("s", far[h:], "f")
+        t2 = pick("v", near, "n") + pick("s", buddy, "b")
+        own = scopy(dst[:, w_dst + rank * per:w_dst + (rank + 1) * per], win.indirect(lists[:, col0 + rank * per16:col0 + (rank + 1) * per16]), "handown", deps)
+        send(far, stage, dst, per, w_dst, k, t1)
+        send(near + buddy, stage, dst, per, w_dst, k, t2)
+        return own
+
+    t_sup = dma("y", T.WB[:, 0:M], T.sup[:], "sup")
+    t_ship = dma("s", T.shipi[:], T.ship[:], "ship")
+    t_hand = dma("s", T.handi[:], T.hand[:], "hand")
+    t_pt = {1: dma("y", T.PT[:, 0:256], T.parts[:, 0:256], "pt1")}
+
+    t_dist = do("g", lambda: g.iota(T.dist[:], [[1, 128]], 128, -1), "dist", [])
+    t_m16 = do("g", lambda: g.iota(T.m16[:], [[0, 8], [1, 16]], 0, 0), "m16", [])
+    t_ones = do("v", lambda: V.memset(T.ones[:], 1.0), "ones", [])
+    t_dm = do("v", lambda: V.tensor_scalar(out=T.dm[:], in0=T.dist[:], scalar1=127, scalar2=None, op0=OP.bitwise_and), "dm", [t_dist])
+    t_s, t_e, t_sf = {}, {}, {}
+    for ld in (1, 2):
+        ta = ts(T["a%d" % ld][:], T.dm[:], ld, OP.is_equal, "a%d" % ld, [t_dm])
+        tk = ts(T["k%d" % ld][:], T.m16[:], ld, OP.is_ge, "k%d" % ld, [t_m16])
+        t_s[ld] = tt(T["sb%d" % ld][:], T["a%d" % ld][:], T["k%d" % ld][:], OP.mult, "sb%d" % ld, [ta, tk])
+        t_e[ld] = tt(T["e%d" % ld][:], T["a%d" % ld][:], T["sb%d" % ld][:], OP.subtract, "e%d" % ld, [t_s[ld]])
+
+    t_ship16 = vcopy(T.ship16[:], T.shipi[:], "ship16", [t_ship])
+    t_own = hand_over(T.WB[:, 0:M], T.ship16, 0, SR, T.SB, T.WB, M, 0, [t_ship16, t_sup])
+
+    wait("y", ("loc0", landed))
+    t_cap, t_st = {}, {}
+    wr = [dma("y", T.C1[127:128, :], T.cap[0:1, :], "capw1"), dma("y", T.C2[126:128, :], T.cap[0:2, :], "capw2")]
+
+    def load_cap(l):
+        b = (l - 1) * A
+        t_cap[l] = wr + [dma("y", T.C1[0:127, b:b + H], T.cap[1:128, b:b + H], "cap1_%d" % l),
+                         dma("y", T.C2[0:126, b + H:b + A], T.cap[2:128, b + H:b + A], "cap2_%d" % l)]
+    load_cap(1)
+    t_st[1] = dma("y", T.ST[:, 0:A], T.stock[:, 0:A], "st1")
+    t_pt[2] = t_pt[3] = dma("y", T.PT[:, 256:768], T.parts[:, 256:768], "pt2")
+    load_cap(2)
+    load_cap(3)
+    t_st[2] = t_st[3] = dma("y", T.ST[:, A:3 * A], T.stock[:, A:3 * A], "st2")
+
+    def sel(out, in_, pat, op, base, cm, role, deps):
+        return do("g", lambda: g.affine_select(out, in_, pat, op, 0.0, base, cm), role, deps)
+    lo, hi = ([[0, 4], [-1, 32]], 15), ([[0, 4], [1, 32]], -16)
+    t_idn = sel(T.idn[:], T.ones[:], [[-1, 128]], OP.is_equal, 0, 1, "idn", [t_ones])
+    t_up = sel(T.up[:], T.ones[:], [[-1, 128]], OP.is_equal, 16, 1, "up", [t_ones])
+    t_dn = sel(T.dn[:], T.ones[:], [[-1, 128]], OP.is_equal, -16, 1, "dn", [t_ones])
+    t_x = [sel(T.x00[:], T.idn[:], lo[0], OP.is_ge, lo[1], 0, "x00", [t_idn]),
+           sel(T.x11[:], T.idn[:], hi[0], OP.is_ge, hi[1], 0, "x11", [t_idn]),
+           sel(T.x01[:], T.up[:], hi[0], OP.is_ge, hi[1], 0, "x01", [t_up]),
+           sel(T.x10[:], T.dn[:], lo[0], OP.is_ge, lo[1], 0, "x10", [t_dn])]
+    X = [[T.x00, T.x01], [T.x10, T.x11]]
+
+    t_cu, t_lists, t_mc = {}, {}, {}
+
+    def prep_first(l):
+        b, c = (l - 1) * 256, (l - 1) * 128
+        t_cu[l] = vcopy(T.cu[:, c:c + 128], T.PT[:, b:b + 128], "cu", [t_pt[l]])
+
+    def prep_lists(l):
+        b, c = (l - 1) * 256, (l - 1) * 128
+        t_lists[l] = []
+        for i in range(4):
+            o, p = slice(c + SLOT[i] * 32, c + SLOT[i] * 32 + 32), b + i * 32
+            t_lists[l].append(vcopy(T.cf[:, o], T.PT[:, p:p + 32], "cf%d" % i, [t_pt[l]]))
+            t_lists[l].append(tt(T.df[:, o], T.PT[:, p + 128:p + 160], T.PT[:, p:p + 32], OP.subtract, "df%d" % i, [t_pt[l]]))
+
+    def prep_cap(l):
+        b = (l - 1) * A
+        t_mc[l] = [ts(T.MC[:, b:b + H], T.C1[:, b:b + H], 0.0, OP.min, "mc1", t_cap[l]),
+                   ts(T.MC[:, b + H:b + A], T.C2[:, b + H:b + A], 0.0, OP.min, "mc2", t_cap[l])]
+
+    prep_first(1)
+    prep_lists(1)
+    t_hand16 = vcopy(T.hand16[:], T.handi[:], "hand16", [t_hand])
+    t_conv = [vcopy(T.W[:, 0:M // 2], T.WB[:, 0:M // 2], "convv", []), scopy(T.W[:, M // 2:M], T.WB[:, M // 2:M], "convs", [])]
+    for ld in (1, 2):
+        t_sf[ld] = vcopy(T["sf%d" % ld][:], T["sb%d" % ld][:], "sf%d" % ld, [t_s[ld]])
+
+    ready = [t_own, t_sup, ("arr0", landed)]
+    t_ev = []
+    for l in range(1, L + 1):
+        raw = l == 1
+        win = (T.WB if raw else T.W)[:, 0:first(l)]
+        G, D = (T.GB, T.DB) if raw else (T.GF, T.DF)
+        XX = (T.XB0, T.XB1) if raw else (T.XF0, T.XF1)
+        c = (l - 1) * 128
+        if raw:
+            on_s, on_v = [(0, 0, 512), (1, 0, 512), (2, 0, 256)], [(3, 0, 512), (2, 256, 512)]
+        else:
+            on_s, on_v = [(0, 0, 512), (1, 0, 512), (2, 0, 256), (2, 256, 512)], [(3, 0, 512)]
+        chunks = []
+        for q, lst in (("s", on_s), ("v", on_v)):
+            for i, a0, a1 in lst:
+                o, li = G[:, i * A + a0:i * A + a1], T.cu[:, c + i * 32 + a0 // 16:c + i * 32 + a1 // 16]
+                tok = (scopy if q == "s" else vcopy)(o, win.indirect(li), "g%s%d_%d" % (q, i, a0), ready + [t_cu[l]])
+                chunks.append((q, i, a0, a1, tok))
+        t_d = []
+        for q, i, a0, a1, tok in [x for x in chunks if x[0] == "v"] + [x for x in chunks if x[0] == "s"]:
+            s = SLOT[i] * A
+            src, dst = G[:, i * A + a0:i * A + a1], D[:, s + a0:s + a1]
+            t_d.append(do("v", lambda: V.transpose(out=dst, in_=src), "d%s%d_%d" % (q, i, a0), [tok]))
+        ev, od = D[:, 15:2 * A:16], D[:, 2 * A + 15:4 * A:16]
+        t_m = tt(T.Mt[:], od, ev, OP.min, "Mt", t_d)
+        t_b = tt(T.Bt[:], od, ev, OP.is_lt, "Bt", t_d)
+        t_g = [tt(T.Gt[:, 0:32], T.Mt[:, 32:64], T.Mt[:, 0:32], OP.is_ge, "Gt0", [t_m]),
+               tt(T.Gt[:, 32:64], T.Mt[:, 32:64], T.Mt[:, 0:32], OP.is_lt, "Gt1", [t_m])]
+        t_h = [tt(T.Hd[:, 0:64], T.Gt[:], T.Bt[:], OP.is_gt, "He", t_g + [t_b]),
+               tt(T.Hd[:, 64:128], T.Gt[:], T.Bt[:], OP.mult, "Ho", t_g + [t_b])]
+        for hb in range(2):
+            for e in range(2):
+                o, w, m = T.PH[:, hb:128:2], X[hb][e], T.Hd[:, e:128:2]
+                t_ph = do("t", lambda: PE.matmul(out=o, lhsT=w[:], rhs=m, start=e == 0, stop=e == 1), ("ph%d" % hb) if e else None, t_h + t_x)
+                if hb == 0 and e:
+                    t_ph0 = t_ph
+        if raw:
+            prep_cap(1)
+        for j, (a0, a1, ld) in enumerate(PIECES):
+            b, P = (l - 1) * A, T["P%d" % j]
+            do("t", lambda: PE.matmul(out=P[:, 0:a1 - a0], lhsT=T.idn[:], rhs=T.ST[:, b + a0:b + a1], start=True, stop=False), None, [t_idn, t_st[l]] + t_ev)
+            do("t", lambda: PE.matmul(out=P[:, 0:a1 - a0], lhsT=T["e%d" % ld][:], rhs=T.MC[:, b + a0:b + a1], start=False, stop=False), None, [t_e[ld]] + t_mc[l])
+        t_t = tt(T.TP[:, 0:128], T.PH[:, 0:128], T.df[:, c:c + 128], OP.mult, "TP", [t_ph0, t_ph] + t_lists[l])
+        t_si = tt(T.SI[:], T.TP[:, 0:128], T.cf[:, c:c + 128], OP.add, "SI", [t_t])
+        t_sel = vcopy(T.sel[:], T.SI[:], "sel", [t_si])
+        h0, h1, ha, hb_ = (0, 256), (256, 512), (256, 384), (384, 512)
+        t_c = {}
+        for s, (a0, a1) in [(0, h0), (1, h0), (0, h1), (2, h0), (1, h1), (3, h0), (2, ha), (2, hb_), (3, ha), (3, hb_)]:
+            b = (l - 1) * A
+            if s == 0:
+                prev, dep = (T.C1 if a1 <= H else T.C2)[:, b + a0:b + a1], t_cap[l]
+            else:
+                prev, dep = XX[(s + 1) % 2][:, a0:a1], [t_c[k] for k in t_c if k[0] == s - 1 and k[1] < a1 and a0 < k[2]]
+            t_c[(s, a0, a1)] = tt(XX[s % 2][:, a0:a1], win.indirect(T.sel[:, s * 32 + a0 // 16:s * 32 + a1 // 16]), prev, OP.min,
+                                  "c%d_%d_%d" % (s, a0, a1), [t_sel] + dep)
+        out, o0 = (T.YB, 0) if l == L else (T.W, first(l))
+        t_ev = []
+        for j, (a0, a1, ld) in enumerate(PIECES):
+            P, w = T["P%d" % j], T[("sb%d" if raw else "sf%d") % ld]
+            t_p = do("t", lambda: PE.matmul(out=P[:, 0:a1 - a0], lhsT=w[:], rhs=XX[1][:, a0:a1], start=False, stop=True), "sh%d" % j,
+                     [t_c[(3, a0, a1)], t_s[ld] if raw else t_sf[ld]])
+            t_ev.append(scopy(out[:, o0 + a0:o0 + a1], P[:, 0:a1 - a0], "ev%d" % j, [t_p]))
+        if l == L:
+            break
+        B = first(l)
+        t_own = hand_over(T.W[:, B:B + A], T.hand16, (l - 1) * 32, SA, T["SH%d" % l], T.W, B + A, l, t_ev + [t_hand16])
+        if raw:
+            m = M + N * SR // 2
+            t_conv += [vcopy(T.W[:, M:m], T.WB[:, M:m], "convv2", []), scopy(T.W[:, m:M + N * SR], T.WB[:, m:M + N * SR], "convs2", [])]
+        prep_first(l + 1)
+        prep_lists(l + 1)
+        prep_cap(l + 1)
+        ready = t_ev + t_conv + [t_own, ("arr%d" % l, landed)]
+    dma("y", T.y[:, 0:H], T.YB[:, 0:H], "y0", [t_ev[0]])
+    dma("y", T.y[:, H:A], T.YB[:, H:A], "y1", t_ev[1:])
+    for k in range(3):
+        wait("g", ("loc%d" % k, landed))
+    for name in total:
+        if best.get(name, 0) < total[name]:
+            wait("g", (name, total[name]))

@@ -4,6 +4,7 @@ from concourse.mybir import AluOpType as OP, ActivationFunctionType as AF
 
 M, A, L, SR, SA, N = 2048, 512, 3, 128, 64, 8
 H = A // 2
+PEN = 8192.0
 
 
 def first(l):
@@ -11,34 +12,39 @@ def first(l):
 
 
 BF, F32, I32, U16 = "bfloat16", "float32", "int32", "uint16"
+NV = 288
 SCRATCH = {
     "WB": ("sbuf", [128, M + N * SR], BF),
     "W": ("sbuf", [128, first(L)], F32),
     "shipi": ("sbuf", [128, 64], I32), "handi": ("sbuf", [128, 64], I32),
     "ship16": ("sbuf", [128, 64], U16), "hand16": ("sbuf", [128, 64], U16),
     "PT": ("sbuf", [128, 768], I32), "cu": ("sbuf", [128, 384], U16),
-    "cf": ("sbuf", [128, 384], F32), "df": ("sbuf", [128, 384], F32),
+    "CF": ("sbuf", [128, 128], F32), "TL": ("sbuf", [128, 128], F32), "VB": ("sbuf", [128, L * NV], F32),
     "SB": ("sbuf", [128, N * SR], BF), "SH1": ("sbuf", [128, N * SA], F32), "SH2": ("sbuf", [128, N * SA], F32),
-    "GB": ("sbuf", [128, 2048], BF), "DB": ("sbuf", [128, 2048], BF),
-    "GF": ("sbuf", [128, 2048], F32), "DF": ("sbuf", [128, 2048], F32),
-    "Bt": ("sbuf", [128, 64], BF), "Mt": ("sbuf", [128, 64], F32), "Gt": ("sbuf", [128, 64], BF), "Hd": ("sbuf", [128, 128], BF),
-    "SI": ("sbuf", [128, 128], F32), "sel": ("sbuf", [128, 128], U16),
+    "GB": ("sbuf", [128, 2 * A], BF), "MB": ("sbuf", [128, 2 * A], BF), "GF": ("sbuf", [128, 2 * A], F32), "MF": ("sbuf", [128, 2 * A], F32),
+    "E": ("sbuf", [128, 192], F32), "BT": ("sbuf", [128, 192], BF), "HT": ("sbuf", [128, 192], BF),
+    "SC": ("sbuf", [128, 256], F32), "RS": ("sbuf", [128, 256], F32), "sel": ("sbuf", [128, 96], U16),
     "XB0": ("sbuf", [128, A], BF), "XB1": ("sbuf", [128, A], BF), "XF0": ("sbuf", [128, A], F32), "XF1": ("sbuf", [128, A], F32),
     "C1": ("sbuf", [128, L * A], BF), "C2": ("sbuf", [128, L * A], BF), "MC": ("sbuf", [128, L * A], BF), "ST": ("sbuf", [128, L * A], BF),
     "YB": ("sbuf", [128, A], F32),
-    "ones": ("sbuf", [128, 128], BF), "dist": ("sbuf", [128, 128], I32), "dm": ("sbuf", [128, 128], I32), "m16": ("sbuf", [128, 128], I32),
+    "dist": ("sbuf", [128, 128], I32), "dm": ("sbuf", [128, 128], I32), "dmb": ("sbuf", [128, 128], I32), "m16": ("sbuf", [128, 128], I32),
+    "bit4": ("sbuf", [128, 128], I32), "dp": ("sbuf", [128, 128], I32), "dq": ("sbuf", [128, 32], I32), "pos": ("sbuf", [128, 32], I32), "posm": ("sbuf", [128, 32], I32),
     "a1": ("sbuf", [128, 128], BF), "a2": ("sbuf", [128, 128], BF), "k1": ("sbuf", [128, 128], BF), "k2": ("sbuf", [128, 128], BF),
     "sb1": ("sbuf", [128, 128], BF), "sb2": ("sbuf", [128, 128], BF), "sf1": ("sbuf", [128, 128], F32), "sf2": ("sbuf", [128, 128], F32),
-    "e1": ("sbuf", [128, 128], BF), "e2": ("sbuf", [128, 128], BF), "idn": ("sbuf", [128, 128], BF),
-    "up": ("sbuf", [128, 128], BF), "dn": ("sbuf", [128, 128], BF),
-    "x00": ("sbuf", [128, 128], BF), "x01": ("sbuf", [128, 128], BF), "x10": ("sbuf", [128, 128], BF), "x11": ("sbuf", [128, 128], BF),
-    "PH": ("psum", [128, 512], F32), "TP": ("psum", [128, 512], F32),
+    "e1": ("sbuf", [128, 128], BF), "e2": ("sbuf", [128, 128], BF), "idn": ("sbuf", [128, 128], BF), "idf": ("sbuf", [128, 128], F32),
+    "x00": ("sbuf", [128, 128], F32), "x01": ("sbuf", [128, 128], F32), "x10": ("sbuf", [128, 128], F32), "x11": ("sbuf", [128, 128], F32),
+    "pmp": ("sbuf", [128, 128], BF), "pmn": ("sbuf", [128, 128], BF), "pm5": ("sbuf", [128, 128], BF),
+    "qb": ("sbuf", [128, 32], BF), "qf": ("sbuf", [128, 32], F32),
+    "PA": ("psum", [128, 512], F32), "PB": ("psum", [128, 512], F32), "PH": ("psum", [128, 512], F32), "PL": ("psum", [128, 512], F32),
     "P0": ("psum", [128, 512], F32), "P1": ("psum", [128, 512], F32), "P2": ("psum", [128, 512], F32),
 }
-NPOOL = 125
+NPOOL = 140
 SEMAPHORES = ["arr0", "arr1", "arr2", "loc0", "loc1", "loc2"] + ["s%d" % i for i in range(NPOOL)]
-SLOT = {0: 0, 2: 1, 1: 2, 3: 3}
 PIECES = [(0, 256, 1), (256, 384, 2), (384, 512, 2)]
+ON_S = [(0, 0, 128), (0, 128, 256), (0, 256, 512), (1, 0, 256), (1, 256, 512)]
+ON_V = [(0, 0, 128), (0, 128, 256), (0, 256, 512), (1, 0, 256), (1, 256, 384), (1, 384, 512)]
+BLOCKS = [("G", 0, 0), ("M", 0, 0), ("G", 0, 1), ("M", 0, 1), ("G", 0, 2), ("G", 0, 3), ("M", 0, 2), ("M", 0, 3),
+          ("G", 1, 0), ("G", 1, 1), ("G", 1, 2), ("G", 1, 3), ("M", 1, 0), ("M", 1, 1), ("M", 1, 2), ("M", 1, 3)]
 
 
 def rank_program(g, core, T, topo):
@@ -69,7 +75,7 @@ def rank_program(g, core, T, topo):
         total[name] = total.get(name, 0) + n
         return (name, total[name])
 
-    V, S, PE, SY = g.vector, g.scalar, g.tensor, g.sync
+    V, S, PE = g.vector, g.scalar, g.tensor
 
     def tt(out, a, b, op, role, deps):
         return do("v", lambda: V.tensor_tensor(out=out, in0=a, in1=b, op=op), role, deps)
@@ -83,8 +89,14 @@ def rank_program(g, core, T, topo):
     def scopy(out, a, role, deps):
         return do("s", lambda: S.activation(out=out, in_=a, func=AF.Copy), role, deps)
 
+    def mm(out, w, m, start, stop, role, deps):
+        return do("t", lambda: PE.matmul(out=out, lhsT=w, rhs=m, start=start, stop=stop), role, deps)
+
     def dma(q, out, in_, role, deps=()):
         return do(q, lambda: Q[q].dma_start(out=out, in_=in_), role, deps, 16)
+
+    def iota(out, pat, base, cm, role):
+        return do("g", lambda: g.iota(out, pat, base, cm), role, [])
 
     here = topo.cores_of(core)
     far = [r for r in range(N) if topo.host(T.cores[r]) != topo.host(core)]
@@ -123,7 +135,6 @@ def rank_program(g, core, T, topo):
 
     def hand_over(win, lists, col0, per, stage, dst, w_dst, k, deps):
         per16 = per // 16
-        toks = {}
 
         def pick(q, ranks, tag):
             got = []
@@ -141,19 +152,34 @@ def rank_program(g, core, T, topo):
 
     t_sup = dma("y", T.WB[:, 0:M], T.sup[:], "sup")
     t_ship = dma("s", T.shipi[:], T.ship[:], "ship")
+    t_pt = {1: dma("s", T.PT[:, 0:256], T.parts[:, 0:256], "pt1")}
     t_hand = dma("s", T.handi[:], T.hand[:], "hand")
-    t_pt = {1: dma("y", T.PT[:, 0:256], T.parts[:, 0:256], "pt1")}
 
-    t_dist = do("g", lambda: g.iota(T.dist[:], [[1, 128]], 128, -1), "dist", [])
-    t_m16 = do("g", lambda: g.iota(T.m16[:], [[0, 8], [1, 16]], 0, 0), "m16", [])
-    t_ones = do("v", lambda: V.memset(T.ones[:], 1.0), "ones", [])
-    t_dm = do("v", lambda: V.tensor_scalar(out=T.dm[:], in0=T.dist[:], scalar1=127, scalar2=None, op0=OP.bitwise_and), "dm", [t_dist])
+    t_dist = iota(T.dist[:], [[1, 128]], 128, -1, "dist")
+    t_bit = iota(T.bit4[:], [[0, 4], [128, 2], [0, 16]], 0, 0, "bit4")
+    t_dp = iota(T.dp[:], [[-4, 8], [-1, 4], [-32, 4]], 0, 1, "dp")
+    t_dq = iota(T.dq[:], [[0, 4], [-16, 8]], -15, 1, "dq")
+    t_m16 = iota(T.m16[:], [[0, 8], [1, 16]], 0, 0, "m16")
+    t_pos = iota(T.pos[:], [[1, 32]], 0, 32, "pos")
+    t_r0 = do("v", lambda: V.memset(T.RS[:], 0.0), "rs0", [])
+    t_rs = do("v", lambda: V.memset(T.RS[:, 0:256:4], -1048576.0), "rs", [t_r0])
+    t_dm = ts(T.dm[:], T.dist[:], 127, OP.bitwise_and, "dm", [t_dist])
+    t_dmb = tt(T.dmb[:], T.dm[:], T.bit4[:], OP.add, "dmb", [t_dm, t_bit])
+    t_x = [ts(T[n][:], T.dmb[:], v, OP.is_equal, n, [t_dmb]) for n, v in (("x00", 0), ("x11", 128), ("x01", 144), ("x10", 112))]
+    X = [[T.x00, T.x01], [T.x10, T.x11]]
+    t_idn = ts(T.idn[:], T.dm[:], 0, OP.is_equal, "idn", [t_dm])
+    t_pm = [do("v", lambda: V.tensor_scalar(out=T[n][:], in0=T.dp[:], scalar1=0, scalar2=v, op0=OP.is_equal, op1=OP.mult), n, [t_dp])
+            for n, v in (("pmp", PEN), ("pmn", -PEN), ("pm5", -512.0))]
+    t_qb = ts(T.qb[:], T.dq[:], 0, OP.is_equal, "qb", [t_dq])
     t_s, t_e, t_sf = {}, {}, {}
     for ld in (1, 2):
         ta = ts(T["a%d" % ld][:], T.dm[:], ld, OP.is_equal, "a%d" % ld, [t_dm])
         tk = ts(T["k%d" % ld][:], T.m16[:], ld, OP.is_ge, "k%d" % ld, [t_m16])
         t_s[ld] = tt(T["sb%d" % ld][:], T["a%d" % ld][:], T["k%d" % ld][:], OP.mult, "sb%d" % ld, [ta, tk])
         t_e[ld] = tt(T["e%d" % ld][:], T["a%d" % ld][:], T["sb%d" % ld][:], OP.subtract, "e%d" % ld, [t_s[ld]])
+    t_posm = ts(T.posm[:], T.pos[:], 511, OP.bitwise_and, "posm", [t_pos])
+    t_idf = scopy(T.idf[:], T.idn[:], "idf", [t_idn])
+    t_qf = scopy(T.qf[:], T.qb[:], "qf", [t_qb])
 
     t_ship16 = vcopy(T.ship16[:], T.shipi[:], "ship16", [t_ship])
     t_own = hand_over(T.WB[:, 0:M], T.ship16, 0, SR, T.SB, T.WB, M, 0, [t_ship16, t_sup])
@@ -173,115 +199,112 @@ def rank_program(g, core, T, topo):
     load_cap(3)
     t_st[2] = t_st[3] = dma("y", T.ST[:, A:3 * A], T.stock[:, A:3 * A], "st2")
 
-    def sel(out, in_, pat, op, base, cm, role, deps):
-        return do("g", lambda: g.affine_select(out, in_, pat, op, 0.0, base, cm), role, deps)
-    lo, hi = ([[0, 4], [-1, 32]], 15), ([[0, 4], [1, 32]], -16)
-    t_idn = sel(T.idn[:], T.ones[:], [[-1, 128]], OP.is_equal, 0, 1, "idn", [t_ones])
-    t_up = sel(T.up[:], T.ones[:], [[-1, 128]], OP.is_equal, 16, 1, "up", [t_ones])
-    t_dn = sel(T.dn[:], T.ones[:], [[-1, 128]], OP.is_equal, -16, 1, "dn", [t_ones])
-    t_x = [sel(T.x00[:], T.idn[:], lo[0], OP.is_ge, lo[1], 0, "x00", [t_idn]),
-           sel(T.x11[:], T.idn[:], hi[0], OP.is_ge, hi[1], 0, "x11", [t_idn]),
-           sel(T.x01[:], T.up[:], hi[0], OP.is_ge, hi[1], 0, "x01", [t_up]),
-           sel(T.x10[:], T.dn[:], lo[0], OP.is_ge, lo[1], 0, "x10", [t_dn])]
-    X = [[T.x00, T.x01], [T.x10, T.x11]]
-
-    t_cu, t_lists, t_mc = {}, {}, {}
+    t_cu, t_pre, t_mc = {}, {}, {}
 
     def prep_first(l):
-        b, c = (l - 1) * 256, (l - 1) * 128
-        t_cu[l] = vcopy(T.cu[:, c:c + 128], T.PT[:, b:b + 128], "cu", [t_pt[l]])
+        b = (l - 1) * 256
+        t_cf = vcopy(T.CF[:], T.PT[:, b:b + 128], "CF", [t_pt[l]])
+        t_tl = do("v", lambda: V.transpose(out=T.TL[:], in_=T.CF[:]), "TL", [t_cf])
+        for i in range(4):
+            for hb in range(2):
+                for e in range(2):
+                    t_pl = mm(T.PL[:, i * 32 + hb:(i + 1) * 32:2], X[hb][e][:], T.TL[:, i * 32 + 16 * e:i * 32 + 16 * e + 16], e == 0, e == 1, "PL", t_x + [t_tl])
+        return t_pl
+
+    def prep_offsets(l, t_pl):
+        c = (l - 1) * 128
+        t_cu[l] = vcopy(T.cu[:, c:c + 128], T.PL[:, 0:128], "cu", [t_pl])
 
     def prep_lists(l):
-        b, c = (l - 1) * 256, (l - 1) * 128
-        t_lists[l] = []
-        for i in range(4):
-            o, p = slice(c + SLOT[i] * 32, c + SLOT[i] * 32 + 32), b + i * 32
-            t_lists[l].append(vcopy(T.cf[:, o], T.PT[:, p:p + 32], "cf%d" % i, [t_pt[l]]))
-            t_lists[l].append(tt(T.df[:, o], T.PT[:, p + 128:p + 160], T.PT[:, p:p + 32], OP.subtract, "df%d" % i, [t_pt[l]]))
+        b, o = (l - 1) * 256, (l - 1) * NV
+        got = []
+        for i, pen in enumerate((0.0, -PEN, -PEN, -2 * PEN)):
+            for k, p in ((0, b + (i ^ 1) * 32), (1, b + 128 + i * 32)):
+                got.append(ts(T.VB[:, o + k * 128 + i:o + (k + 1) * 128:4], T.PT[:, p:p + 32], pen, OP.add, "vb%d%d" % (k, i), [t_pt[l]]))
+        got.append(ts(T.VB[:, o + 256:o + NV], T.posm[:], 512.0, OP.add, "vbm", [t_posm]))
+        t_pre[l] = mm(T.PH[:, 0:NV], T.idf[:], T.VB[:, o:o + NV], True, False, "pre", got + [t_idf])
 
     def prep_cap(l):
         b = (l - 1) * A
         t_mc[l] = [ts(T.MC[:, b:b + H], T.C1[:, b:b + H], 0.0, OP.min, "mc1", t_cap[l]),
                    ts(T.MC[:, b + H:b + A], T.C2[:, b + H:b + A], 0.0, OP.min, "mc2", t_cap[l])]
 
-    prep_first(1)
+    t_pl = prep_first(1)
     prep_lists(1)
+    prep_offsets(1, t_pl)
     t_hand16 = vcopy(T.hand16[:], T.handi[:], "hand16", [t_hand])
-    t_conv = [vcopy(T.W[:, 0:M // 2], T.WB[:, 0:M // 2], "convv", []), scopy(T.W[:, M // 2:M], T.WB[:, M // 2:M], "convs", [])]
     for ld in (1, 2):
-        t_sf[ld] = vcopy(T["sf%d" % ld][:], T["sb%d" % ld][:], "sf%d" % ld, [t_s[ld]])
+        t_sf[ld] = scopy(T["sf%d" % ld][:], T["sb%d" % ld][:], "sf%d" % ld, [t_s[ld]])
+    t_conv = [scopy(T.W[:, 0:M // 2], T.WB[:, 0:M // 2], "convs", [])]
 
     ready = [t_own, t_sup, ("arr0", landed)]
     t_ev = []
     for l in range(1, L + 1):
         raw = l == 1
         win = (T.WB if raw else T.W)[:, 0:first(l)]
-        G, D = (T.GB, T.DB) if raw else (T.GF, T.DF)
+        G, MN = (T.GB, T.MB) if raw else (T.GF, T.MF)
         XX = (T.XB0, T.XB1) if raw else (T.XF0, T.XF1)
         c = (l - 1) * 128
-        if raw:
-            on_s, on_v = [(0, 0, 512), (1, 0, 512), (2, 0, 256)], [(3, 0, 512), (2, 256, 512)]
-        else:
-            on_s, on_v = [(0, 0, 512), (1, 0, 512), (2, 0, 256), (2, 256, 512)], [(3, 0, 512)]
-        chunks = []
-        for q, lst in (("s", on_s), ("v", on_v)):
-            for i, a0, a1 in lst:
-                o, li = G[:, i * A + a0:i * A + a1], T.cu[:, c + i * 32 + a0 // 16:c + i * 32 + a1 // 16]
-                tok = (scopy if q == "s" else vcopy)(o, win.indirect(li), "g%s%d_%d" % (q, i, a0), ready + [t_cu[l]])
-                chunks.append((q, i, a0, a1, tok))
-        t_d = []
-        for q, i, a0, a1, tok in [x for x in chunks if x[0] == "v"] + [x for x in chunks if x[0] == "s"]:
-            s = SLOT[i] * A
-            src, dst = G[:, i * A + a0:i * A + a1], D[:, s + a0:s + a1]
-            t_d.append(do("v", lambda: V.transpose(out=dst, in_=src), "d%s%d_%d" % (q, i, a0), [tok]))
-        ev, od = D[:, 15:2 * A:16], D[:, 2 * A + 15:4 * A:16]
-        t_m = tt(T.Mt[:], od, ev, OP.min, "Mt", t_d)
-        t_b = tt(T.Bt[:], od, ev, OP.is_lt, "Bt", t_d)
-        t_g = [tt(T.Gt[:, 0:32], T.Mt[:, 32:64], T.Mt[:, 0:32], OP.is_ge, "Gt0", [t_m]),
-               tt(T.Gt[:, 32:64], T.Mt[:, 32:64], T.Mt[:, 0:32], OP.is_lt, "Gt1", [t_m])]
-        t_h = [tt(T.Hd[:, 0:64], T.Gt[:], T.Bt[:], OP.is_gt, "He", t_g + [t_b]),
-               tt(T.Hd[:, 64:128], T.Gt[:], T.Bt[:], OP.mult, "Ho", t_g + [t_b])]
-        for hb in range(2):
-            for e in range(2):
-                o, w, m = T.PH[:, hb:128:2], X[hb][e], T.Hd[:, e:128:2]
-                t_ph = do("t", lambda: PE.matmul(out=o, lhsT=w[:], rhs=m, start=e == 0, stop=e == 1), ("ph%d" % hb) if e else None, t_h + t_x)
-                if hb == 0 and e:
-                    t_ph0 = t_ph
+        t_g, t_m = {}, {}
+        for p, a0, a1 in ON_S:
+            li = T.cu[:, c + 2 * p * 32 + a0 // 16:c + 2 * p * 32 + a1 // 16]
+            t_g[(p, a0, a1)] = scopy(G[:, p * A + a0:p * A + a1], win.indirect(li), "g%d_%d" % (p, a0), ready + [t_cu[l]])
+        for p, a0, a1 in ON_V:
+            li = T.cu[:, c + (2 * p + 1) * 32 + a0 // 16:c + (2 * p + 1) * 32 + a1 // 16]
+            t_m[(p, a0, a1)] = tt(MN[:, p * A + a0:p * A + a1], win.indirect(li), G[:, p * A + a0:p * A + a1], OP.min, "m%d_%d" % (p, a0),
+                                  ready + [t_cu[l]] + [t_g[k] for k in t_g if k[0] == p and k[1] < a1 and a0 < k[2]])
+        q = T.qb if raw else T.qf
+        for kind, p, y in BLOCKS:
+            toks, src = (t_g, G) if kind == "G" else (t_m, MN)
+            dep = [toks[k] for k in toks if k[0] == p and k[1] <= 128 * y < k[2]] + [t_qb if raw else t_qf]
+            w = src[:, p * A + 128 * y:p * A + 128 * y + 128]
+            if (kind, p) == ("M", 1):
+                t_pb = mm(T.PB[:, y:128:4], w, q[:, 0:32], True, True, "PB", dep)
+            else:
+                o = {("G", 1): 0, ("M", 0): 64, ("G", 0): 128}[(kind, p)]
+                t_pa = mm(T.PA[:, o + y:o + 64:4], w, q[:, 0:16], True, True, "PA", dep)
+        t_E = scopy(T.E[:], T.PA[:, 0:192], "E", [t_pa])
+        t_b = [tt(T.BT[:, 128:192], T.E[:, 128:192], T.E[:, 64:128], OP.is_gt, "b01", [t_E]),
+               tt(T.BT[:, 0:128], T.E[:, 0:128], T.PB[:, 0:128], OP.is_gt, "b23", [t_E, t_pb])]
+        t_ht = do("v", lambda: V.transpose(out=T.HT[:], in_=T.BT[:]), "HT", t_b)
         if raw:
             prep_cap(1)
+        for i, w, b in ((0, T.pmn, 128), (1, T.pmp, 128), (2, T.pmn, 0), (3, T.pmp, 0), (0, T.pmn, 64), (1, T.pmn, 64), (2, T.pmp, 64), (3, T.pmp, 64)):
+            mm(T.PH[:, i:256:4], w[:], T.HT[:, b:b + 64], False, False, "PH", [t_ht, t_pre[l]] + t_pm)
+        t_ph = mm(T.PH[:, 256:NV], T.pm5[:], T.HT[:, 64:96], False, True, "PH", [])
         for j, (a0, a1, ld) in enumerate(PIECES):
             b, P = (l - 1) * A, T["P%d" % j]
-            do("t", lambda: PE.matmul(out=P[:, 0:a1 - a0], lhsT=T.idn[:], rhs=T.ST[:, b + a0:b + a1], start=True, stop=False), None, [t_idn, t_st[l]] + t_ev)
-            do("t", lambda: PE.matmul(out=P[:, 0:a1 - a0], lhsT=T["e%d" % ld][:], rhs=T.MC[:, b + a0:b + a1], start=False, stop=False), None, [t_e[ld]] + t_mc[l])
-        t_t = tt(T.TP[:, 0:128], T.PH[:, 0:128], T.df[:, c:c + 128], OP.mult, "TP", [t_ph0, t_ph] + t_lists[l])
-        t_si = tt(T.SI[:], T.TP[:, 0:128], T.cf[:, c:c + 128], OP.add, "SI", [t_t])
-        t_sel = vcopy(T.sel[:], T.SI[:], "sel", [t_si])
+            mm(P[:, 0:a1 - a0], T.idn[:], T.ST[:, b + a0:b + a1], True, False, None, [t_idn, t_st[l]] + t_ev)
+            mm(P[:, 0:a1 - a0], T["e%d" % ld][:], T.MC[:, b + a0:b + a1], False, False, None, [t_e[ld]] + t_mc[l])
+        t_sc = do("v", lambda: V.tensor_tensor_scan(out=T.SC[:], data0=T.RS[:], data1=T.PH[:, 0:256], initial=0.0, op0=OP.add, op1=OP.max), "SC", [t_ph, t_rs])
+        t_selm = vcopy(T.sel[:, 64:96], T.PH[:, 256:NV], "selm", [t_ph])
+        t_sel = vcopy(T.sel[:, 0:64], T.SC[:, 3:256:4], "sel", [t_sc])
         h0, h1, ha, hb_ = (0, 256), (256, 512), (256, 384), (384, 512)
         t_c = {}
-        for s, (a0, a1) in [(0, h0), (1, h0), (0, h1), (2, h0), (1, h1), (3, h0), (2, ha), (2, hb_), (3, ha), (3, hb_)]:
+        for s, (a0, a1) in [(0, h0), (0, h1), (1, h0), (1, h1), (2, h0), (2, ha), (2, hb_)]:
             b = (l - 1) * A
             if s == 0:
-                prev, dep = (T.C1 if a1 <= H else T.C2)[:, b + a0:b + a1], t_cap[l]
+                prev, dep = (T.C1 if a1 <= H else T.C2)[:, b + a0:b + a1], t_cap[l] + [t_selm]
             else:
-                prev, dep = XX[(s + 1) % 2][:, a0:a1], [t_c[k] for k in t_c if k[0] == s - 1 and k[1] < a1 and a0 < k[2]]
-            t_c[(s, a0, a1)] = tt(XX[s % 2][:, a0:a1], win.indirect(T.sel[:, s * 32 + a0 // 16:s * 32 + a1 // 16]), prev, OP.min,
-                                  "c%d_%d_%d" % (s, a0, a1), [t_sel] + dep)
+                prev, dep = XX[(s + 1) % 2][:, a0:a1], [t_sel] + [t_c[k] for k in t_c if k[0] == s - 1 and k[1] < a1 and a0 < k[2]]
+            wn, o = ((MN[:, 0:2 * A], 64), (win, 32), (win, 0))[s]
+            t_c[(s, a0, a1)] = tt(XX[s % 2][:, a0:a1], wn.indirect(T.sel[:, o + a0 // 16:o + a1 // 16]), prev, OP.min, "c%d_%d_%d" % (s, a0, a1), dep)
         out, o0 = (T.YB, 0) if l == L else (T.W, first(l))
         t_ev = []
         for j, (a0, a1, ld) in enumerate(PIECES):
             P, w = T["P%d" % j], T[("sb%d" if raw else "sf%d") % ld]
-            t_p = do("t", lambda: PE.matmul(out=P[:, 0:a1 - a0], lhsT=w[:], rhs=XX[1][:, a0:a1], start=False, stop=True), "sh%d" % j,
-                     [t_c[(3, a0, a1)], t_s[ld] if raw else t_sf[ld]])
+            t_p = mm(P[:, 0:a1 - a0], w[:], XX[0][:, a0:a1], False, True, "sh%d" % j, [t_c[(2, a0, a1)], t_s[ld] if raw else t_sf[ld]])
             t_ev.append(scopy(out[:, o0 + a0:o0 + a1], P[:, 0:a1 - a0], "ev%d" % j, [t_p]))
         if l == L:
             break
         B = first(l)
         t_own = hand_over(T.W[:, B:B + A], T.hand16, (l - 1) * 32, SA, T["SH%d" % l], T.W, B + A, l, t_ev + [t_hand16])
+        t_pl = prep_first(l + 1)
         if raw:
-            m = M + N * SR // 2
-            t_conv += [vcopy(T.W[:, M:m], T.WB[:, M:m], "convv2", []), scopy(T.W[:, m:M + N * SR], T.WB[:, m:M + N * SR], "convs2", [])]
-        prep_first(l + 1)
+            m = M + N * SR
+            t_conv += [scopy(T.W[:, M // 2:m - 512], T.WB[:, M // 2:m - 512], "convs2", []), vcopy(T.W[:, m - 512:m], T.WB[:, m - 512:m], "convv2", [])]
         prep_lists(l + 1)
+        prep_offsets(l + 1, t_pl)
         prep_cap(l + 1)
         ready = t_ev + t_conv + [t_own, ("arr%d" % l, landed)]
     dma("y", T.y[:, 0:H], T.YB[:, 0:H], "y0", [t_ev[0]])

import numpy as np
from concourse.bass import DstId, RemoteDMATransfer
from concourse.mybir import AluOpType as OP, ActivationFunctionType as AF

M, A, L, SR, SA, N = 2048, 512, 3, 128, 64, 8
H = A // 2
PEN = 8192.0


def first(l):
    return M + N * SR + (l - 1) * (A + N * SA)


BF, F32, I32, U16 = "bfloat16", "float32", "int32", "uint16"
NV = 288
SCRATCH = {
    "WB": ("sbuf", [128, M + N * SR], BF),
    "W": ("sbuf", [128, first(L)], F32),
    "shipi": ("sbuf", [128, 64], I32), "handi": ("sbuf", [128, 64], I32),
    "ship16": ("sbuf", [128, 64], U16), "hand16": ("sbuf", [128, 64], U16),
    "PT": ("sbuf", [128, 768], I32), "cu": ("sbuf", [128, 384], U16),
    "CF": ("sbuf", [128, 128], F32), "TL": ("sbuf", [128, 128], F32), "VB": ("sbuf", [128, L * NV], F32),
    "SB": ("sbuf", [128, N * SR], BF), "SH1": ("sbuf", [128, N * SA], F32), "SH2": ("sbuf", [128, N * SA], F32),
    "GB": ("sbuf", [128, 2 * A], BF), "MB": ("sbuf", [128, 2 * A], BF), "GF": ("sbuf", [128, 2 * A], F32), "MF": ("sbuf", [128, 2 * A], F32),
    "E": ("sbuf", [128, 192], F32), "BT": ("sbuf", [128, 192], BF), "HT": ("sbuf", [128, 192], BF),
    "SC": ("sbuf", [128, 256], F32), "RS": ("sbuf", [128, 256], F32), "sel": ("sbuf", [128, 96], U16),
    "XB0": ("sbuf", [128, A], BF), "XB1": ("sbuf", [128, A], BF), "XF0": ("sbuf", [128, A], F32), "XF1": ("sbuf", [128, A], F32),
    "C1": ("sbuf", [128, L * A], BF), "C2": ("sbuf", [128, L * A], BF), "MC": ("sbuf", [128, L * A], BF), "ST": ("sbuf", [128, L * A], BF),
    "YB": ("sbuf", [128, A], F32),
    "dist": ("sbuf", [128, 128], I32), "dm": ("sbuf", [128, 128], I32), "dmb": ("sbuf", [128, 128], I32), "m16": ("sbuf", [128, 128], I32),
    "bit4": ("sbuf", [128, 128], I32), "dp": ("sbuf", [128, 128], I32), "dq": ("sbuf", [128, 32], I32), "pos": ("sbuf", [128, 32], I32), "posm": ("sbuf", [128, 32], I32),
    "a1": ("sbuf", [128, 128], BF), "a2": ("sbuf", [128, 128], BF), "k1": ("sbuf", [128, 128], BF), "k2": ("sbuf", [128, 128], BF),
    "sb1": ("sbuf", [128, 128], BF), "sb2": ("sbuf", [128, 128], BF), "sf1": ("sbuf", [128, 128], F32), "sf2": ("sbuf", [128, 128], F32),
    "e1": ("sbuf", [128, 128], BF), "e2": ("sbuf", [128, 128], BF), "idn": ("sbuf", [128, 128], BF), "idf": ("sbuf", [128, 128], F32),
    "x00": ("sbuf", [128, 128], F32), "x01": ("sbuf", [128, 128], F32), "x10": ("sbuf", [128, 128], F32), "x11": ("sbuf", [128, 128], F32),
    "pmp": ("sbuf", [128, 128], BF), "pmn": ("sbuf", [128, 128], BF), "pm5": ("sbuf", [128, 128], BF),
    "qb": ("sbuf", [128, 32], BF), "qf": ("sbuf", [128, 32], F32),
    "PA": ("psum", [128, 512], F32), "PB": ("psum", [128, 512], F32), "PH": ("psum", [128, 512], F32), "PL": ("psum", [128, 512], F32),
    "P0": ("psum", [128, 512], F32), "P1": ("psum", [128, 512], F32), "P2": ("psum", [128, 512], F32),
}
NPOOL = 140
SEMAPHORES = ["arr0", "arr1", "arr2", "loc0", "loc1", "loc2"] + ["s%d" % i for i in range(NPOOL)]
PIECES = [(0, 256, 1), (256, 384, 2), (384, 512, 2)]
ON_S = [(0, 0, 128), (0, 128, 256), (0, 256, 512), (1, 0, 256), (1, 256, 512)]
ON_V = [(0, 0, 128), (0, 128, 256), (0, 256, 512), (1, 0, 256), (1, 256, 384), (1, 384, 512)]
BLOCKS = [("G", 0, 0), ("M", 0, 0), ("G", 0, 1), ("M", 0, 1), ("G", 0, 2), ("G", 0, 3), ("M", 0, 2), ("M", 0, 3),
          ("G", 1, 0), ("G", 1, 1), ("G", 1, 2), ("G", 1, 3), ("M", 1, 0), ("M", 1, 1), ("M", 1, 2), ("M", 1, 3)]


def rank_program(g, core, T, topo):
    rank = T.rank_of(core)
    if rank is None:
        return
    Q = {"v": g.vector, "s": g.scalar, "t": g.tensor, "g": g, "y": g.sync}
    pool, total, seen, best = {}, {}, {q: {} for q in Q}, {}

    def wait(q, tok):
        name, val = tok
        if seen[q].get(name, 0) >= val:
            return
        Q[q].wait_ge(T.sem[name], val)
        seen[q][name] = val
        best[name] = max(best.get(name, 0), val)

    def do(q, fn, role, deps, n=1):
        for d in deps:
            wait(q, d)
        inst = fn()
        if role is None:
            return None
        if role not in pool:
            pool[role] = "s%d" % len(pool)
        name = pool[role]
        inst.then_inc(T.sem[name], n)
        total[name] = total.get(name, 0) + n
        return (name, total[name])

    V, S, PE = g.vector, g.scalar, g.tensor

    def tt(out, a, b, op, role, deps):
        return do("v", lambda: V.tensor_tensor(out=out, in0=a, in1=b, op=op), role, deps)

    def ts(out, a, s1, op, role, deps):
        return do("v", lambda: V.tensor_scalar(out=out, in0=a, scalar1=s1, scalar2=None, op0=op), role, deps)

    def vcopy(out, a, role, deps):
        return do("v", lambda: V.tensor_copy(out=out, in_=a), role, deps)

    def scopy(out, a, role, deps):
        return do("s", lambda: S.activation(out=out, in_=a, func=AF.Copy), role, deps)

    def mm(out, w, m, start, stop, role, deps):
        return do("t", lambda: PE.matmul(out=out, lhsT=w, rhs=m, start=start, stop=stop), role, deps)

    def dma(q, out, in_, role, deps=()):
        return do(q, lambda: Q[q].dma_start(out=out, in_=in_), role, deps, 16)

    def iota(out, pat, base, cm, role):
        return do("g", lambda: g.iota(out, pat, base, cm), role, [])

    here = topo.cores_of(core)
    far = [r for r in range(N) if topo.host(T.cores[r]) != topo.host(core)]
    buddy = [r for r in range(N) if T.cores[r] in here and r != rank]
    near = [r for r in range(N) if r not in far and r not in buddy and r != rank]
    off = topo.engines(core, T.cores[far[0]])
    rest = [e for e in topo.engines(core, T.cores[buddy[0]]) if e not in off]
    share = {}
    for grp in (far, near):
        k = len(off) // len(grp)
        for j, r in enumerate(grp):
            share[r] = off[j * k:(j + 1) * k]
    for j, r in enumerate(buddy):
        share[r] = rest[4 * j:4 * j + 4:2]
    landed = sum(len(v) for v in share.values())

    def send(ranks, src, dst, w_src, w_dst, k, deps):
        for d in deps:
            wait("g", d)
        tr = []
        for r in ranks:
            rid, pid = topo.addr(T.cores[r], core)
            tr.append(RemoteDMATransfer(src=src[:, r * w_src:(r + 1) * w_src], dst=dst[:, w_dst + rank * w_src:w_dst + (rank + 1) * w_src],
                                        dst_ids=[DstId(rid=rid, pnc=pid)], dma_engine_mask=sum(1 << e for e in share[r]),
                                        remote_sem=T.sem["arr%d" % k]))
        g.remote_dma_fused(tr, local_sem=T.sem["loc%d" % k])

    def runs(ranks):
        out = []
        for r in ranks:
            if out and out[-1][1] == r:
                out[-1][1] = r + 1
            else:
                out.append([r, r + 1])
        return out

    def hand_over(win, lists, col0, per, stage, dst, w_dst, k, deps):
        per16 = per // 16

        def pick(q, ranks, tag):
            got = []
            for j, (b, e) in enumerate(runs(ranks)):
                o, i = stage[:, b * per:e * per], win.indirect(lists[:, col0 + b * per16:col0 + e * per16])
                got.append((vcopy if q == "v" else scopy)(o, i, "hand%s%s%d" % (q, tag, j), deps))
            return got
        h = len(far) // 2
        t1 = pick("v", far[:h], "f") + pick("s", far[h:], "f")
        t2 = pick("v", near, "n") + pick("s", buddy, "b")
        own = scopy(dst[:, w_dst + rank * per:w_dst + (rank + 1) * per], win.indirect(lists[:, col0 + rank * per16:col0 + (rank + 1) * per16]), "handown", deps)
        send(far, stage, dst, per, w_dst, k, t1)
        send(near + buddy, stage, dst, per, w_dst, k, t2)
        return own

    t_sup = dma("y", T.WB[:, 0:M], T.sup[:], "sup")
    t_ship = dma("s", T.shipi[:], T.ship[:], "ship")
    t_pt = {1: dma("s", T.PT[:, 0:256], T.parts[:, 0:256], "pt1")}
    t_hand = dma("s", T.handi[:], T.hand[:], "hand")

    t_dist = iota(T.dist[:], [[1, 128]], 128, -1, "dist")
    t_bit = iota(T.bit4[:], [[0, 4], [128, 2], [0, 16]], 0, 0, "bit4")
    t_dp = iota(T.dp[:], [[-4, 8], [-1, 4], [-32, 4]], 0, 1, "dp")
    t_dq = iota(T.dq[:], [[0, 4], [-16, 8]], -15, 1, "dq")
    t_m16 = iota(T.m16[:], [[0, 8], [1, 16]], 0, 0, "m16")
    t_pos = iota(T.pos[:], [[1, 32]], 0, 32, "pos")
    t_r0 = do("v", lambda: V.memset(T.RS[:], 0.0), "rs0", [])
    t_rs = do("v", lambda: V.memset(T.RS[:, 0:256:4], -1048576.0), "rs", [t_r0])
    t_dm = ts(T.dm[:], T.dist[:], 127, OP.bitwise_and, "dm", [t_dist])
    t_dmb = tt(T.dmb[:], T.dm[:], T.bit4[:], OP.add, "dmb", [t_dm, t_bit])
    t_x = [ts(T[n][:], T.dmb[:], v, OP.is_equal, n, [t_dmb]) for n, v in (("x00", 0), ("x11", 128), ("x01", 144), ("x10", 112))]
    X = [[T.x00, T.x01], [T.x10, T.x11]]
    t_idn = ts(T.idn[:], T.dm[:], 0, OP.is_equal, "idn", [t_dm])
    t_pm = [do("v", lambda: V.tensor_scalar(out=T[n][:], in0=T.dp[:], scalar1=0, scalar2=v, op0=OP.is_equal, op1=OP.mult), n, [t_dp])
            for n, v in (("pmp", PEN), ("pmn", -PEN), ("pm5", -512.0))]
    t_qb = ts(T.qb[:], T.dq[:], 0, OP.is_equal, "qb", [t_dq])
    t_s, t_e, t_sf = {}, {}, {}
    for ld in (1, 2):
        ta = ts(T["a%d" % ld][:], T.dm[:], ld, OP.is_equal, "a%d" % ld, [t_dm])
        tk = ts(T["k%d" % ld][:], T.m16[:], ld, OP.is_ge, "k%d" % ld, [t_m16])
        t_s[ld] = tt(T["sb%d" % ld][:], T["a%d" % ld][:], T["k%d" % ld][:], OP.mult, "sb%d" % ld, [ta, tk])
        t_e[ld] = tt(T["e%d" % ld][:], T["a%d" % ld][:], T["sb%d" % ld][:], OP.subtract, "e%d" % ld, [t_s[ld]])
    t_posm = ts(T.posm[:], T.pos[:], 511, OP.bitwise_and, "posm", [t_pos])
    t_idf = scopy(T.idf[:], T.idn[:], "idf", [t_idn])
    t_qf = scopy(T.qf[:], T.qb[:], "qf", [t_qb])

    t_ship16 = vcopy(T.ship16[:], T.shipi[:], "ship16", [t_ship])
    t_own = hand_over(T.WB[:, 0:M], T.ship16, 0, SR, T.SB, T.WB, M, 0, [t_ship16, t_sup])

    wait("y", ("loc0", landed))
    t_cap, t_st = {}, {}
    wr = [dma("y", T.C1[127:128, :], T.cap[0:1, :], "capw1"), dma("y", T.C2[126:128, :], T.cap[0:2, :], "capw2")]

    def load_cap(l):
        b = (l - 1) * A
        t_cap[l] = wr + [dma("y", T.C1[0:127, b:b + H], T.cap[1:128, b:b + H], "cap1_%d" % l),
                         dma("y", T.C2[0:126, b + H:b + A], T.cap[2:128, b + H:b + A], "cap2_%d" % l)]
    load_cap(1)
    t_st[1] = dma("y", T.ST[:, 0:A], T.stock[:, 0:A], "st1")
    t_pt[2] = t_pt[3] = dma("y", T.PT[:, 256:768], T.parts[:, 256:768], "pt2")
    load_cap(2)
    load_cap(3)
    t_st[2] = t_st[3] = dma("y", T.ST[:, A:3 * A], T.stock[:, A:3 * A], "st2")

    t_cu, t_pre, t_mc = {}, {}, {}

    def prep_first(l):
        b = (l - 1) * 256
        t_cf = vcopy(T.CF[:], T.PT[:, b:b + 128], "CF", [t_pt[l]])
        t_tl = do("v", lambda: V.transpose(out=T.TL[:], in_=T.CF[:]), "TL", [t_cf])
        for i in range(4):
            for hb in range(2):
                for e in range(2):
                    t_pl = mm(T.PL[:, i * 32 + hb:(i + 1) * 32:2], X[hb][e][:], T.TL[:, i * 32 + 16 * e:i * 32 + 16 * e + 16], e == 0, e == 1, "PL", t_x + [t_tl])
        return t_pl

    def prep_offsets(l, t_pl):
        c = (l - 1) * 128
        t_cu[l] = vcopy(T.cu[:, c:c + 128], T.PL[:, 0:128], "cu", [t_pl])

    def prep_lists(l):
        b, o = (l - 1) * 256, (l - 1) * NV
        got = []
        for i, pen in enumerate((0.0, -PEN, -PEN, -2 * PEN)):
            for k, p in ((0, b + (i ^ 1) * 32), (1, b + 128 + i * 32)):
                got.append(ts(T.VB[:, o + k * 128 + i:o + (k + 1) * 128:4], T.PT[:, p:p + 32], pen, OP.add, "vb%d%d" % (k, i), [t_pt[l]]))
        got.append(ts(T.VB[:, o + 256:o + NV], T.posm[:], 512.0, OP.add, "vbm", [t_posm]))
        t_pre[l] = mm(T.PH[:, 0:NV], T.idf[:], T.VB[:, o:o + NV], True, False, "pre", got + [t_idf])

    def prep_cap(l):
        b = (l - 1) * A
        t_mc[l] = [ts(T.MC[:, b:b + H], T.C1[:, b:b + H], 0.0, OP.min, "mc1", t_cap[l]),
                   ts(T.MC[:, b + H:b + A], T.C2[:, b + H:b + A], 0.0, OP.min, "mc2", t_cap[l])]

    t_pl = prep_first(1)
    prep_lists(1)
    prep_offsets(1, t_pl)
    t_hand16 = vcopy(T.hand16[:], T.handi[:], "hand16", [t_hand])
    for ld in (1, 2):
        t_sf[ld] = scopy(T["sf%d" % ld][:], T["sb%d" % ld][:], "sf%d" % ld, [t_s[ld]])
    t_conv = [scopy(T.W[:, 0:M // 2], T.WB[:, 0:M // 2], "convs", [])]

    ready = [t_own, t_sup, ("arr0", landed)]
    t_ev = []
    for l in range(1, L + 1):
        raw = l == 1
        win = (T.WB if raw else T.W)[:, 0:first(l)]
        G, MN = (T.GB, T.MB) if raw else (T.GF, T.MF)
        XX = (T.XB0, T.XB1) if raw else (T.XF0, T.XF1)
        c = (l - 1) * 128
        t_g, t_m = {}, {}
        for p, a0, a1 in ON_S:
            li = T.cu[:, c + 2 * p * 32 + a0 // 16:c + 2 * p * 32 + a1 // 16]
            t_g[(p, a0, a1)] = scopy(G[:, p * A + a0:p * A + a1], win.indirect(li), "g%d_%d" % (p, a0), ready + [t_cu[l]])
        for p, a0, a1 in ON_V:
            li = T.cu[:, c + (2 * p + 1) * 32 + a0 // 16:c + (2 * p + 1) * 32 + a1 // 16]
            t_m[(p, a0, a1)] = tt(MN[:, p * A + a0:p * A + a1], win.indirect(li), G[:, p * A + a0:p * A + a1], OP.min, "m%d_%d" % (p, a0),
                                  ready + [t_cu[l]] + [t_g[k] for k in t_g if k[0] == p and k[1] < a1 and a0 < k[2]])
        q = T.qb if raw else T.qf
        for kind, p, y in BLOCKS:
            toks, src = (t_g, G) if kind == "G" else (t_m, MN)
            dep = [toks[k] for k in toks if k[0] == p and k[1] <= 128 * y < k[2]] + [t_qb if raw else t_qf]
            w = src[:, p * A + 128 * y:p * A + 128 * y + 128]
            if (kind, p) == ("M", 1):
                t_pb = mm(T.PB[:, y:128:4], w, q[:, 0:32], True, True, "PB", dep)
            else:
                o = {("G", 1): 0, ("M", 0): 64, ("G", 0): 128}[(kind, p)]
                t_pa = mm(T.PA[:, o + y:o + 64:4], w, q[:, 0:16], True, True, "PA", dep)
        t_E = scopy(T.E[:], T.PA[:, 0:192], "E", [t_pa])
        t_b = [tt(T.BT[:, 128:192], T.E[:, 128:192], T.E[:, 64:128], OP.is_gt, "b01", [t_E]),
               tt(T.BT[:, 0:128], T.E[:, 0:128], T.PB[:, 0:128], OP.is_gt, "b23", [t_E, t_pb])]
        t_ht = do("v", lambda: V.transpose(out=T.HT[:], in_=T.BT[:]), "HT", t_b)
        if raw:
            prep_cap(1)
        for i, w, b in ((0, T.pmn, 128), (1, T.pmp, 128), (2, T.pmn, 0), (3, T.pmp, 0), (0, T.pmn, 64), (1, T.pmn, 64), (2, T.pmp, 64), (3, T.pmp, 64)):
            mm(T.PH[:, i:256:4], w[:], T.HT[:, b:b + 64], False, False, "PH", [t_ht, t_pre[l]] + t_pm)
        t_ph = mm(T.PH[:, 256:NV], T.pm5[:], T.HT[:, 64:96], False, True, "PH", [])
        for j, (a0, a1, ld) in enumerate(PIECES):
            b, P = (l - 1) * A, T["P%d" % j]
            mm(P[:, 0:a1 - a0], T.idn[:], T.ST[:, b + a0:b + a1], True, False, None, [t_idn, t_st[l]] + t_ev)
            mm(P[:, 0:a1 - a0], T["e%d" % ld][:], T.MC[:, b + a0:b + a1], False, False, None, [t_e[ld]] + t_mc[l])
        t_sc = do("v", lambda: V.tensor_tensor_scan(out=T.SC[:], data0=T.RS[:], data1=T.PH[:, 0:256], initial=0.0, op0=OP.add, op1=OP.max), "SC", [t_ph, t_rs])
        t_selm = vcopy(T.sel[:, 64:96], T.PH[:, 256:NV], "selm", [t_ph])
        t_sel = vcopy(T.sel[:, 0:64], T.SC[:, 3:256:4], "sel", [t_sc])
        h0, h1, ha, hb_ = (0, 256), (256, 512), (256, 384), (384, 512)
        t_c = {}
        for s, (a0, a1) in [(0, h0), (0, h1), (1, h0), (1, h1), (2, h0), (2, ha), (2, hb_)]:
            b = (l - 1) * A
            if s == 0:
                prev, dep = (T.C1 if a1 <= H else T.C2)[:, b + a0:b + a1], t_cap[l] + [t_selm]
            else:
                prev, dep = XX[(s + 1) % 2][:, a0:a1], [t_sel] + [t_c[k] for k in t_c if k[0] == s - 1 and k[1] < a1 and a0 < k[2]]
            wn, o = ((MN[:, 0:2 * A], 64), (win, 32), (win, 0))[s]
            t_c[(s, a0, a1)] = tt(XX[s % 2][:, a0:a1], wn.indirect(T.sel[:, o + a0 // 16:o + a1 // 16]), prev, OP.min, "c%d_%d_%d" % (s, a0, a1), dep)
        out, o0 = (T.YB, 0) if l == L else (T.W, first(l))
        t_ev = []
        for j, (a0, a1, ld) in enumerate(PIECES):
            P, w = T["P%d" % j], T[("sb%d" if raw else "sf%d") % ld]
            t_p = mm(P[:, 0:a1 - a0], w[:], XX[0][:, a0:a1], False, True, "sh%d" % j, [t_c[(2, a0, a1)], t_s[ld] if raw else t_sf[ld]])
            t_ev.append(scopy(out[:, o0 + a0:o0 + a1], P[:, 0:a1 - a0], "ev%d" % j, [t_p]))
        if l == L:
            break
        B = first(l)
        t_own = hand_over(T.W[:, B:B + A], T.hand16, (l - 1) * 32, SA, T["SH%d" % l], T.W, B + A, l, t_ev + [t_hand16])
        t_pl = prep_first(l + 1)
        if raw:
            m = M + N * SR
            t_conv += [scopy(T.W[:, M // 2:m - 512], T.WB[:, M // 2:m - 512], "convs2", []), vcopy(T.W[:, m - 512:m], T.WB[:, m - 512:m], "convv2", [])]
        prep_lists(l + 1)
        prep_offsets(l + 1, t_pl)
        prep_cap(l + 1)
        ready = t_ev + t_conv + [t_own, ("arr%d" % l, landed)]
    dma("y", T.y[:, 0:H], T.YB[:, 0:H], "y0", [t_ev[0]])
    dma("y", T.y[:, H:A], T.YB[:, H:A], "y1", t_ev[1:])
    for k in range(3):
        wait("g", ("loc%d" % k, landed))
    for name in total:
        if best.get(name, 0) < total[name]:
            wait("g", (name, total[name]))
